import numpy as np
import ml_dtypes


def mxq(x, axis, fmt="e4m3"):
    dtype, down = {"e4m3": (ml_dtypes.float8_e4m3fn, 7), "e5m2": (ml_dtypes.float8_e5m2, 14)}[fmt]
    v = np.moveaxis(np.asarray(x, np.float32).astype(ml_dtypes.bfloat16).astype(np.float64), axis, -1)
    blocks = v.reshape(v.shape[:-1] + (-1, 32))
    amax = np.abs(blocks).max(-1, keepdims=True)
    byte = np.maximum(np.where(amax > 0, np.frexp(amax)[1] - 1 + 127, 0) - down, 1)
    scale = np.exp2(byte - 127.0)
    codes = (blocks / scale).astype(np.float32).astype(dtype).astype(np.float64)
    return np.moveaxis((codes * scale).reshape(v.shape), -1, axis)


WIDE = False


def mx_kscale(k):
    if not WIDE:
        return np.ones(k)
    levels = np.array([10, -10, 5, -5, 0])
    if k % 512:
        return np.exp2(np.random.permutation(np.resize(levels, k // 32))).repeat(32)
    a = np.empty((k // 512, 16))
    for p in range(k // 512):
        a[p, :8] = np.random.permutation(np.resize(levels, 8))
        for g in range(8):
            far = levels[np.abs(levels - a[p, g]) >= 10]
            a[p, g + 8] = far[np.random.randint(len(far))]
    return np.exp2(a.ravel()).repeat(32)


def f64(x):
    return np.asarray(x).astype(np.float64)


def striped(idx):
    return np.tile(idx.reshape(-1, 16).T, (8, 1)).astype(np.uint16)


def unstriped(offs):
    return offs[:16].T.reshape(-1).astype(np.int64)


def pack_weight(w):
    k, n = w.shape
    w = f64(np.asarray(w, np.float32).astype(ml_dtypes.bfloat16)).reshape(k // 32, 32, n)
    amax = np.abs(w).max(1)
    byte = np.clip(np.where(amax > 0, np.frexp(amax)[1] - 1 + 127 - 7, 1), 1, 254)
    scaled = (w * np.exp2(127.0 - byte)[:, None, :]).reshape(k, n).astype(np.float32)
    words = np.ascontiguousarray(scaled.reshape(k // 512, 128, 4, n).transpose(0, 1, 3, 2)).astype(ml_dtypes.float8_e4m3fn).view(np.uint8)
    return words, np.ascontiguousarray(byte.astype(np.uint8).reshape(k // 512, 16, n))


def unpack_weight(words, scales):
    g, p, n, _ = words.shape
    vals = np.ascontiguousarray(words).view(ml_dtypes.float8_e4m3fn).astype(np.float64) * np.repeat(np.exp2(scales.astype(np.float64) - 127.0), 8, axis=1)[..., None]
    return vals.transpose(0, 1, 3, 2).reshape(g * 512, n)


K, T, S, N, H, U = 512, 2048, 512, 128, 512, 1024


def setup_inputs():
    n = np.random.standard_normal
    s = mx_kscale(K)[:, None]
    u = mx_kscale(H)
    packed_xT = pack_weight(n((K, T)) * s)
    return {
        "x_words": packed_xT[0],
        "x_scales": packed_xT[1],
        "w1": (n((K, H)) / np.sqrt(K) / s).astype(np.float32),
        "w2": (n((K, H)) / np.sqrt(K) / s).astype(np.float32),
        "unit": (np.random.uniform(0.6, 1.4, (H, 1)) * u[:, None]).astype(np.float32),
        "w3": (n((H, N)) / np.sqrt(H) / u[:, None]).astype(np.float32),
        "offs": striped(np.random.permutation(T)[:S]),
        "ask1": striped(np.random.permutation(np.concatenate([np.arange(S), np.random.randint(0, S, U - S)]))),
        "ask2": striped(np.random.permutation(np.concatenate([np.arange(S), np.random.randint(0, S, U - S)]))),
    }


def reference(x_words, x_scales, w1, w2, unit, w3, offs, ask1, ask2):
    xq = unpack_weight(x_words, x_scales)[:, unstriped(offs)]
    y = mxq(f64(w1), 0, "e4m3").T @ xq
    ya = y[:, unstriped(ask1)]
    yb_ = y[:, unstriped(ask2)]
    best = np.minimum(ya, yb_)
    z1 = mxq(f64(w2), 0, "e4m3").T @ xq
    za = z1[:, unstriped(ask1)]
    zb_ = z1[:, unstriped(ask2)]
    hid = f64(unit) * (best - np.maximum(za, zb_))
    return mxq(f64(w3), 0, "e4m3").T @ mxq(hid, 0, "e4m3")

@@ -1,0 +1,222 @@
+from contextlib import ExitStack
+
+import concourse.mybir as mybir
+
+F32 = mybir.dt.float32
+BF16 = mybir.dt.bfloat16
+I32 = mybir.dt.int32
+U32 = mybir.dt.uint32
+U16 = mybir.dt.uint16
+U8 = mybir.dt.uint8
+FP8X4 = mybir.dt.float8_e4m3fn_x4
+ALU = mybir.AluOpType
+COPY = mybir.ActivationFunctionType.Copy
+
+K, T, S, N, H, U = 512, 2048, 512, 128, 512, 1024
+FLOPS = 2 * (2 * K * H * S + H * N * U)
+
+P = 128
+PACK = 4
+LIST_ROWS = 16
+
+FUSED_CHUNKS = [(0, 384), (384, 384)]
+COPIED_CHUNKS = [(768, 128), (896, 128)]
+
+
+def tile_picked_ypeerlo_spr_p_kernel(tc, x_words, x_scales, w1, w2, unit, w3, offs, ask1, ask2, out):
+    nc = tc.nc
+    with ExitStack() as ctx:
+        keep = ctx.enter_context(tc.tile_pool(name="keep", bufs=1))
+        ring = ctx.enter_context(tc.tile_pool(name="ring", bufs=4))
+        pair = ctx.enter_context(tc.tile_pool(name="pair", bufs=2))
+        psum = ctx.enter_context(tc.psum_pool(name="psum", bufs=8))
+
+        offs_sb = keep.tile([P, S // LIST_ROWS], U16)
+        ask1_sb = keep.tile([P, U // LIST_ROWS], U16)
+        ask2_sb = keep.tile([P, U // LIST_ROWS], U16)
+        xw = keep.tile([P, T], I32, align_bytes=64)
+        xs = keep.tile([P, T], U8, align_bytes=64)
+        w2_raw = keep.tile([P, PACK, H], F32)
+        w1_raw = keep.tile([P, PACK, H], F32)
+        w3_raw = keep.tile([P, PACK, N], F32)
+        unit_sb = keep.tile([P, PACK], F32)
+
+        nc.vector.memset(xs[:].bitcast(I32), 0)
+        nc.sync.dma_start(offs_sb[:], offs)
+        nc.sync.dma_start(xw[:], x_words[0].rearrange("p n t -> p (n t)").bitcast(I32))
+        for q in range(4):
+            nc.scalar.dma_start(xs[32 * q : 32 * q + 4, :].bitcast(I32), x_scales[0, 4 * q : 4 * q + 4, :].bitcast(I32))
+        nc.gpsimd.dma_start(unit_sb[:], unit.rearrange("(p t) o -> p (t o)", t=PACK))
+        nc.sync.dma_start(w2_raw[:], w2.rearrange("(p j) c -> p j c", j=PACK))
+        nc.sync.dma_start(ask1_sb[:], ask1)
+        nc.sync.dma_start(ask2_sb[:], ask2)
+        nc.sync.dma_start(w1_raw[:], w1.rearrange("(p j) c -> p j c", j=PACK))
+        nc.sync.dma_start(w3_raw[:], w3.rearrange("(p t) n -> p t n", t=PACK))
+
+        size = keep.tile([P, PACK], F32)
+        neg_size = keep.tile([P, PACK], F32)
+        twice = keep.tile([P, PACK], F32)
+        sgn = keep.tile([P, PACK], F32)
+        nc.vector.scalar_tensor_tensor(neg_size[:], unit_sb[:], -1.0, unit_sb[:], ALU.mult, ALU.min)
+        nc.vector.scalar_tensor_tensor(size[:], unit_sb[:], -1.0, unit_sb[:], ALU.mult, ALU.max)
+        nc.vector.tensor_scalar(twice[:], unit_sb[:], 0.0, 2.0, ALU.is_ge, ALU.mult)
+        nc.vector.tensor_scalar(sgn[:], twice[:], 1.0, -1.0, ALU.mult, ALU.add)
+
+        xg_scales = keep.tile([P, S], U8, align_bytes=64)
+        xg_words = keep.tile([P, S], U32, align_bytes=64)
+        nc.vector.tensor_copy(xg_scales[:], xs[:].indirect(offs_sb[:]))
+        nc.vector.tensor_copy(xg_words[:], xw[:].bitcast(U32).indirect(offs_sb[:]))
+
+        def weight_tiles(name):
+            grouped = keep.tile([P, PACK, P, PACK], BF16, align_bytes=64, name=name + "_bf")
+            codes = keep.tile([P, H], U32, align_bytes=64, name=name + "_codes")
+            scales = keep.tile([P, H], U8, align_bytes=64, name=name + "_scales")
+            return grouped, codes, scales
+
+        def cast_weight(raw, grouped, t0, t1):
+            nc.vector.tensor_copy(
+                grouped[:, t0:t1].rearrange("p t m j -> p m j t"),
+                raw[:].rearrange("p j (m t) -> p m j t", t=PACK)[:, :, :, t0:t1],
+            )
+
+        def quantise_weight(grouped, codes, scales, t0, t1):
+            nc.vector.quantize_mx(
+                out=codes[:, t0 * P : t1 * P].bitcast(FP8X4),
+                scales=scales[:, t0 * P : t1 * P],
+                in_=grouped[:, t0:t1].rearrange("p t m j -> p (t m j)"),
+            )
+
+        def product(codes, scales, t):
+            acc = psum.tile([P, S], F32, name="acc")
+            nc.tensor.matmul_mx(
+                out=acc[:],
+                lhsT=codes[:, t * P : (t + 1) * P].bitcast(FP8X4),
+                lhsT_scale=scales[:, t * P : (t + 1) * P],
+                rhs=xg_words[:].bitcast(FP8X4),
+                rhs_scale=xg_scales[:],
+                start=True,
+                stop=True,
+            )
+            return acc
+
+        def evict(acc, factor, t, name):
+            window = keep.tile([P, S], F32, name=name + str(t))
+            nc.scalar.activation(window[:], acc[:], COPY, scale=factor[:, t : t + 1])
+            return window
+
+        def entries(lst, r0, n):
+            return lst[:, r0 // LIST_ROWS : (r0 + n) // LIST_ROWS]
+
+        w2_bf, w2_codes, w2_scales = weight_tiles("w2")
+        w1_bf, w1_codes, w1_scales = weight_tiles("w1")
+        cast_weight(w2_raw, w2_bf, 0, 1)
+        quantise_weight(w2_bf, w2_codes, w2_scales, 0, 1)
+        z_acc = [product(w2_codes, w2_scales, 0)]
+        cast_weight(w2_raw, w2_bf, 1, PACK)
+        quantise_weight(w2_bf, w2_codes, w2_scales, 1, PACK)
+        for t in range(1, PACK):
+            z_acc.append(product(w2_codes, w2_scales, t))
+        cast_weight(w1_raw, w1_bf, 0, 1)
+        quantise_weight(w1_bf, w1_codes, w1_scales, 0, 1)
+        y_acc = [product(w1_codes, w1_scales, 0)]
+        cast_weight(w1_raw, w1_bf, 1, PACK)
+        quantise_weight(w1_bf, w1_codes, w1_scales, 1, PACK)
+        for t in range(1, PACK):
+            y_acc.append(product(w1_codes, w1_scales, t))
+
+        w3_bf = keep.tile([P, N, PACK], BF16, align_bytes=64)
+        w3_codes = keep.tile([P, N], U32, align_bytes=64)
+        w3_scales = keep.tile([P, N], U8, align_bytes=64)
+
+        def prepare_w3():
+            nc.vector.tensor_tensor(
+                w3_bf[:].rearrange("p (c e) t -> p c t e", e=2),
+                w3_raw[:].rearrange("p t (c e) -> p c t e", e=2),
+                sgn[:].unsqueeze(1).unsqueeze(3).to_broadcast([P, N // 2, PACK, 2]),
+                ALU.mult,
+            )
+            nc.vector.quantize_mx(
+                out=w3_codes[:].bitcast(FP8X4), scales=w3_scales[:], in_=w3_bf[:].rearrange("p n t -> p (n t)")
+            )
+
+        hid_bf = keep.tile([P, U, PACK], BF16, align_bytes=64)
+        hid_codes = keep.tile([P, U], U32, align_bytes=64)
+        hid_scales = keep.tile([P, U], U8, align_bytes=64)
+
+        def combine(left, right, op, r0, n):
+            nc.vector.tensor_tensor(
+                hid_bf[:, r0 : r0 + n, :].rearrange("p (c e) t -> p c t e", e=2),
+                left.rearrange("p t (c e) -> p c t e", e=2),
+                right.rearrange("p t (c e) -> p c t e", e=2),
+                op,
+            )
+
+        def quantise_hid(r0, n):
+            nc.vector.quantize_mx(
+                out=hid_codes[:, r0 : r0 + n].bitcast(FP8X4),
+                scales=hid_scales[:, r0 : r0 + n],
+                in_=hid_bf[:, r0 : r0 + n, :].rearrange("p n t -> p (n t)"),
+            )
+
+        def finish(r0, n):
+            acc = psum.tile([P, S], F32, name="acc")
+            done = 0
+            while done < n:
+                width = 256 if n - done >= 256 else 128
+                cols = slice(r0 + done, r0 + done + width)
+                nc.tensor.matmul_mx(
+                    out=acc[:, done : done + width],
+                    lhsT=w3_codes[:].bitcast(FP8X4),
+                    lhsT_scale=w3_scales[:],
+                    rhs=hid_codes[:, cols].bitcast(FP8X4),
+                    rhs_scale=hid_scales[:, cols],
+                    start=True,
+                    stop=True,
+                )
+                done = done + width
+            staged = keep.tile([P, n], F32, name="staged" + str(r0))
+            nc.scalar.copy(staged[:], acc[:, :n])
+            nc.sync.dma_start(out[:, r0 : r0 + n], staged[:])
+
+        z_win = []
+        y_win = []
+        pending = None
+        for c, (r0, n) in enumerate(FUSED_CHUNKS):
+            first = pair.tile([P, PACK, n], F32, name="first")
+            second = pair.tile([P, PACK, n], F32, name="second")
+            for t in range(PACK):
+                if c == 0:
+                    z_win.append(evict(z_acc[t], neg_size, t, "z"))
+                bids = ring.tile([P, 2, n], F32, name="bids")
+                nc.scalar.activation(bids[:, 0, :], z_win[t][:].indirect(entries(ask1_sb, r0, n)), COPY)
+                nc.scalar.activation(bids[:, 1, :], z_win[t][:].indirect(entries(ask2_sb, r0, n)), COPY)
+                if c == 0:
+                    y_win.append(evict(y_acc[t], size, t, "y"))
+                low = ring.tile([P, n], F32, name="low")
+                nc.vector.tensor_tensor(low[:], bids[:, 0, :], bids[:, 1, :], ALU.min)
+                if pending is not None and t == 0:
+                    quantise_hid(*pending)
+                nc.vector.tensor_tensor(first[:, t, :], y_win[t][:].indirect(entries(ask1_sb, r0, n)), low[:], ALU.add)
+                nc.vector.tensor_tensor(second[:, t, :], y_win[t][:].indirect(entries(ask2_sb, r0, n)), low[:], ALU.add)
+                if c == 0 and t == 0:
+                    prepare_w3()
+            if pending is not None:
+                finish(*pending)
+            combine(first[:], second[:], ALU.min, r0, n)
+            pending = (r0, n)
+
+        for r0, n in COPIED_CHUNKS:
+            lows = pair.tile([P, PACK, 2, n], F32, name="lows")
+            for t in range(PACK):
+                both = ring.tile([P, 2, 2, n], F32, name="both")
+                for side, lst in enumerate((ask1_sb, ask2_sb)):
+                    for which, win in enumerate((z_win, y_win)):
+                        nc.scalar.activation(both[:, side, which, :], win[t][:].indirect(entries(lst, r0, n)), COPY)
+                nc.vector.tensor_tensor(lows[:, t], both[:, 0], both[:, 1], ALU.min)
+                if t == 0:
+                    quantise_hid(*pending)
+            finish(*pending)
+            combine(lows[:, :, 0, :], lows[:, :, 1, :], ALU.add, r0, n)
+            pending = (r0, n)
+        quantise_hid(*pending)
+        finish(*pending)

@@ -19,8 +19,10 @@ P = 128
 PACK = 4
 LIST_ROWS = 16
 
-FUSED_CHUNKS = [(0, 384), (384, 384)]
-COPIED_CHUNKS = [(768, 128), (896, 128)]
+FUSED = 768
+COPIED = U - FUSED
+WINDOW = FUSED + LIST_ROWS
+FIRST_PIECE = 256
 
 
 def tile_picked_ypeerlo_spr_p_kernel(tc, x_words, x_scales, w1, w2, unit, w3, offs, ask1, ask2, out):
@@ -36,22 +38,26 @@ def tile_picked_ypeerlo_spr_p_kernel(tc, x_words, x_scales, w1, w2, unit, w3, of
         ask2_sb = keep.tile([P, U // LIST_ROWS], U16)
         xw = keep.tile([P, T], I32, align_bytes=64)
         xs = keep.tile([P, T], U8, align_bytes=64)
-        w2_raw = keep.tile([P, PACK, H], F32)
+        w2_raw = keep.tile([P, PACK, H], F32, name="shared_raw")
         w1_raw = keep.tile([P, PACK, H], F32)
-        w3_raw = keep.tile([P, PACK, N], F32)
         unit_sb = keep.tile([P, PACK], F32)
 
-        nc.vector.memset(xs[:].bitcast(I32), 0)
+        nc.gpsimd.memset(xs[:].bitcast(I32), 0)
         nc.sync.dma_start(offs_sb[:], offs)
-        nc.sync.dma_start(xw[:], x_words[0].rearrange("p n t -> p (n t)").bitcast(I32))
-        for q in range(4):
-            nc.scalar.dma_start(xs[32 * q : 32 * q + 4, :].bitcast(I32), x_scales[0, 4 * q : 4 * q + 4, :].bitcast(I32))
-        nc.gpsimd.dma_start(unit_sb[:], unit.rearrange("(p t) o -> p (t o)", t=PACK))
+        nc.scalar.dma_start(unit_sb[:], unit.rearrange("(p t) o -> p (t o)", t=PACK))
         nc.sync.dma_start(w2_raw[:], w2.rearrange("(p j) c -> p j c", j=PACK))
+        for q in range(4):
+            nc.sync.dma_start(xs[32 * q : 32 * q + 4, :].bitcast(I32), x_scales[0, 4 * q : 4 * q + 4, :].bitcast(I32))
+        nc.sync.dma_start(xw[:], x_words[0].rearrange("p n t -> p (n t)").bitcast(I32))
         nc.sync.dma_start(ask1_sb[:], ask1)
         nc.sync.dma_start(ask2_sb[:], ask2)
         nc.sync.dma_start(w1_raw[:], w1.rearrange("(p j) c -> p j c", j=PACK))
-        nc.sync.dma_start(w3_raw[:], w3.rearrange("(p t) n -> p t n", t=PACK))
+
+        z_win = [keep.tile([P, WINDOW], F32, name="z" + str(t)) for t in range(PACK)]
+        y_win = [keep.tile([P, WINDOW], F32, name="y" + str(t)) for t in range(PACK)]
+        for t in range(PACK):
+            nc.gpsimd.memset(z_win[t][:, S:], 0.0)
+            nc.gpsimd.memset(y_win[t][:, S:], 0.0)
 
         size = keep.tile([P, PACK], F32)
         neg_size = keep.tile([P, PACK], F32)
@@ -64,8 +70,6 @@ def tile_picked_ypeerlo_spr_p_kernel(tc, x_words, x_scales, w1, w2, unit, w3, of
 
         xg_scales = keep.tile([P, S], U8, align_bytes=64)
         xg_words = keep.tile([P, S], U32, align_bytes=64)
-        nc.vector.tensor_copy(xg_scales[:], xs[:].indirect(offs_sb[:]))
-        nc.vector.tensor_copy(xg_words[:], xw[:].bitcast(U32).indirect(offs_sb[:]))
 
         def weight_tiles(name):
             grouped = keep.tile([P, PACK, P, PACK], BF16, align_bytes=64, name=name + "_bf")
@@ -73,8 +77,8 @@ def tile_picked_ypeerlo_spr_p_kernel(tc, x_words, x_scales, w1, w2, unit, w3, of
             scales = keep.tile([P, H], U8, align_bytes=64, name=name + "_scales")
             return grouped, codes, scales
 
-        def cast_weight(raw, grouped, t0, t1):
-            nc.vector.tensor_copy(
+        def cast_weight(copy, raw, grouped, t0, t1):
+            copy(
                 grouped[:, t0:t1].rearrange("p t m j -> p m j t"),
                 raw[:].rearrange("p j (m t) -> p m j t", t=PACK)[:, :, :, t0:t1],
             )
@@ -86,44 +90,51 @@ def tile_picked_ypeerlo_spr_p_kernel(tc, x_words, x_scales, w1, w2, unit, w3, of
                 in_=grouped[:, t0:t1].rearrange("p t m j -> p (t m j)"),
             )
 
-        def product(codes, scales, t):
+        def product(codes, scales, t, cols):
             acc = psum.tile([P, S], F32, name="acc")
             nc.tensor.matmul_mx(
-                out=acc[:],
+                out=acc[:, cols],
                 lhsT=codes[:, t * P : (t + 1) * P].bitcast(FP8X4),
                 lhsT_scale=scales[:, t * P : (t + 1) * P],
-                rhs=xg_words[:].bitcast(FP8X4),
-                rhs_scale=xg_scales[:],
+                rhs=xg_words[:, cols].bitcast(FP8X4),
+                rhs_scale=xg_scales[:, cols],
                 start=True,
                 stop=True,
             )
             return acc
 
-        def evict(acc, factor, t, name):
-            window = keep.tile([P, S], F32, name=name + str(t))
-            nc.scalar.activation(window[:], acc[:], COPY, scale=factor[:, t : t + 1])
-            return window
+        def evict(window, acc, factor, t):
+            nc.scalar.activation(window[t][:, :S], acc[t][:], COPY, scale=factor[:, t : t + 1])
 
         def entries(lst, r0, n):
             return lst[:, r0 // LIST_ROWS : (r0 + n) // LIST_ROWS]
 
         w2_bf, w2_codes, w2_scales = weight_tiles("w2")
         w1_bf, w1_codes, w1_scales = weight_tiles("w1")
-        cast_weight(w2_raw, w2_bf, 0, 1)
-        quantise_weight(w2_bf, w2_codes, w2_scales, 0, 1)
-        z_acc = [product(w2_codes, w2_scales, 0)]
-        cast_weight(w2_raw, w2_bf, 1, PACK)
-        quantise_weight(w2_bf, w2_codes, w2_scales, 1, PACK)
-        for t in range(1, PACK):
-            z_acc.append(product(w2_codes, w2_scales, t))
-        cast_weight(w1_raw, w1_bf, 0, 1)
+        cast_weight(nc.vector.tensor_copy, w2_raw, w2_bf, 0, 2)
+        cast_weight(nc.scalar.copy, w2_raw, w2_bf, 2, PACK)
+        nc.vector.tensor_copy(xg_scales[:], xs[:].indirect(offs_sb[:]))
+        quantise_weight(w2_bf, w2_codes, w2_scales, 0, PACK)
+        for half in range(2):
+            cols = slice(half * S // 2, (half + 1) * S // 2)
+            picks = entries(offs_sb, half * S // 2, S // 2)
+            nc.vector.tensor_copy(xg_words[:, cols], xw[:].bitcast(U32).indirect(picks))
+            acc = product(w2_codes, w2_scales, 0, cols)
+            nc.scalar.activation(z_win[0][:, cols], acc[:, cols], COPY, scale=neg_size[:, 0:1])
+        every = slice(0, S)
+        z_acc = {t: product(w2_codes, w2_scales, t, every) for t in range(1, PACK)}
+        nc.vector.tensor_scalar(z_win[1][:, :S], z_acc[1][:], neg_size[:, 1:2], None, ALU.mult)
+        cast_weight(nc.vector.tensor_copy, w1_raw, w1_bf, 0, 1)
         quantise_weight(w1_bf, w1_codes, w1_scales, 0, 1)
-        y_acc = [product(w1_codes, w1_scales, 0)]
-        cast_weight(w1_raw, w1_bf, 1, PACK)
+        y_acc = {0: product(w1_codes, w1_scales, 0, every)}
+        cast_weight(nc.vector.tensor_copy, w1_raw, w1_bf, 1, PACK)
+        nc.vector.tensor_scalar(y_win[0][:, :S], y_acc[0][:], size[:, 0:1], None, ALU.mult)
         quantise_weight(w1_bf, w1_codes, w1_scales, 1, PACK)
         for t in range(1, PACK):
-            y_acc.append(product(w1_codes, w1_scales, t))
+            y_acc[t] = product(w1_codes, w1_scales, t, every)
 
+        w3_raw = keep.tile([P, PACK, N], F32, name="shared_raw")
+        nc.sync.dma_start(w3_raw[:], w3.rearrange("(p t) n -> p t n", t=PACK))
         w3_bf = keep.tile([P, N, PACK], BF16, align_bytes=64)
         w3_codes = keep.tile([P, N], U32, align_bytes=64)
         w3_scales = keep.tile([P, N], U8, align_bytes=64)
@@ -160,63 +171,67 @@ def tile_picked_ypeerlo_spr_p_kernel(tc, x_words, x_scales, w1, w2, unit, w3, of
 
         def finish(r0, n):
             acc = psum.tile([P, S], F32, name="acc")
-            done = 0
-            while done < n:
-                width = 256 if n - done >= 256 else 128
-                cols = slice(r0 + done, r0 + done + width)
-                nc.tensor.matmul_mx(
-                    out=acc[:, done : done + width],
-                    lhsT=w3_codes[:].bitcast(FP8X4),
-                    lhsT_scale=w3_scales[:],
-                    rhs=hid_codes[:, cols].bitcast(FP8X4),
-                    rhs_scale=hid_scales[:, cols],
-                    start=True,
-                    stop=True,
-                )
-                done = done + width
+            cols = slice(r0, r0 + n)
+            nc.tensor.matmul_mx(
+                out=acc[:, :n],
+                lhsT=w3_codes[:].bitcast(FP8X4),
+                lhsT_scale=w3_scales[:],
+                rhs=hid_codes[:, cols].bitcast(FP8X4),
+                rhs_scale=hid_scales[:, cols],
+                start=True,
+                stop=True,
+            )
             staged = keep.tile([P, n], F32, name="staged" + str(r0))
             nc.scalar.copy(staged[:], acc[:, :n])
-            nc.sync.dma_start(out[:, r0 : r0 + n], staged[:])
+            nc.sync.dma_start(out[:, cols], staged[:])
 
-        z_win = []
-        y_win = []
-        pending = None
-        for c, (r0, n) in enumerate(FUSED_CHUNKS):
-            first = pair.tile([P, PACK, n], F32, name="first")
-            second = pair.tile([P, PACK, n], F32, name="second")
-            for t in range(PACK):
-                if c == 0:
-                    z_win.append(evict(z_acc[t], neg_size, t, "z"))
-                bids = ring.tile([P, 2, n], F32, name="bids")
-                nc.scalar.activation(bids[:, 0, :], z_win[t][:].indirect(entries(ask1_sb, r0, n)), COPY)
-                nc.scalar.activation(bids[:, 1, :], z_win[t][:].indirect(entries(ask2_sb, r0, n)), COPY)
-                if c == 0:
-                    y_win.append(evict(y_acc[t], size, t, "y"))
-                low = ring.tile([P, n], F32, name="low")
-                nc.vector.tensor_tensor(low[:], bids[:, 0, :], bids[:, 1, :], ALU.min)
-                if pending is not None and t == 0:
-                    quantise_hid(*pending)
-                nc.vector.tensor_tensor(first[:, t, :], y_win[t][:].indirect(entries(ask1_sb, r0, n)), low[:], ALU.add)
-                nc.vector.tensor_tensor(second[:, t, :], y_win[t][:].indirect(entries(ask2_sb, r0, n)), low[:], ALU.add)
-                if c == 0 and t == 0:
-                    prepare_w3()
-            if pending is not None:
-                finish(*pending)
-            combine(first[:], second[:], ALU.min, r0, n)
-            pending = (r0, n)
+        first = keep.tile([P, PACK, FUSED], F32)
+        second = keep.tile([P, PACK, FUSED], F32)
 
-        for r0, n in COPIED_CHUNKS:
-            lows = pair.tile([P, PACK, 2, n], F32, name="lows")
-            for t in range(PACK):
-                both = ring.tile([P, 2, 2, n], F32, name="both")
+        def fused_piece(t, r0, n):
+            bids = ring.tile([P, 2, n], F32, name="fetched")
+            nc.scalar.activation(bids[:, 0, :], z_win[t][:].indirect(entries(ask1_sb, r0, n)), COPY)
+            nc.scalar.activation(bids[:, 1, :], z_win[t][:].indirect(entries(ask2_sb, r0, n)), COPY)
+            if r0 == 0 and t > 0:
+                evict(y_win, y_acc, size, t)
+            low = pair.tile([P, n], F32, name="low")
+            nc.vector.tensor_tensor(low[:], bids[:, 0, :], bids[:, 1, :], ALU.min)
+            cols = slice(r0, r0 + n)
+            nc.vector.tensor_tensor(first[:, t, cols], y_win[t][:].indirect(entries(ask1_sb, r0, n)), low[:], ALU.add)
+            nc.vector.tensor_tensor(second[:, t, cols], y_win[t][:].indirect(entries(ask2_sb, r0, n)), low[:], ALU.add)
+
+        for t in range(PACK):
+            if t > 1:
+                evict(z_win, z_acc, neg_size, t)
+            if t == 0:
+                fused_piece(t, 0, FIRST_PIECE)
+                fused_piece(t, FIRST_PIECE, FUSED - FIRST_PIECE)
+                prepare_w3()
+            else:
+                fused_piece(t, 0, FUSED)
+
+        lows = keep.tile([P, PACK, 2, COPIED], F32)
+
+        def copied_piece(t):
+            both = ring.tile([P, 2, 2, COPIED], F32, name="fetched")
+            for which, win in enumerate((z_win, y_win)):
                 for side, lst in enumerate((ask1_sb, ask2_sb)):
-                    for which, win in enumerate((z_win, y_win)):
-                        nc.scalar.activation(both[:, side, which, :], win[t][:].indirect(entries(lst, r0, n)), COPY)
-                nc.vector.tensor_tensor(lows[:, t], both[:, 0], both[:, 1], ALU.min)
-                if t == 0:
-                    quantise_hid(*pending)
-            finish(*pending)
-            combine(lows[:, :, 0, :], lows[:, :, 1, :], ALU.add, r0, n)
-            pending = (r0, n)
-        quantise_hid(*pending)
-        finish(*pending)
+                    nc.scalar.activation(both[:, side, which, :], win[t][:].indirect(entries(lst, FUSED, COPIED)), COPY)
+            nc.vector.tensor_tensor(lows[:, t], both[:, 0], both[:, 1], ALU.min)
+
+        combine(first[:, :, :512], second[:, :, :512], ALU.min, 0, 512)
+        copied_piece(0)
+        copied_piece(1)
+        quantise_hid(0, 512)
+        combine(first[:, :, 512:], second[:, :, 512:], ALU.min, 512, 256)
+        copied_piece(2)
+        quantise_hid(512, 256)
+        copied_piece(3)
+        finish(0, 512)
+        finish(512, 256)
+        combine(lows[:, :, 0, :128], lows[:, :, 1, :128], ALU.add, 768, 128)
+        combine(lows[:, :, 0, 128:], lows[:, :, 1, 128:], ALU.add, 896, 128)
+        quantise_hid(768, 128)
+        quantise_hid(896, 128)
+        finish(768, 128)
+        finish(896, 128)

@@ -19,17 +19,17 @@ P = 128
 PACK = 4
 LIST_ROWS = 16
 
-FUSED = 768
+FUSED = 736
 COPIED = U - FUSED
 WINDOW = FUSED + LIST_ROWS
-FIRST_PIECE = 256
+FIRST_PIECE = 384
 
 
 def tile_picked_ypeerlo_spr_p_kernel(tc, x_words, x_scales, w1, w2, unit, w3, offs, ask1, ask2, out):
     nc = tc.nc
     with ExitStack() as ctx:
         keep = ctx.enter_context(tc.tile_pool(name="keep", bufs=1))
-        ring = ctx.enter_context(tc.tile_pool(name="ring", bufs=4))
+        ring = ctx.enter_context(tc.tile_pool(name="ring", bufs=3))
         pair = ctx.enter_context(tc.tile_pool(name="pair", bufs=2))
         psum = ctx.enter_context(tc.psum_pool(name="psum", bufs=8))
 
@@ -38,7 +38,8 @@ def tile_picked_ypeerlo_spr_p_kernel(tc, x_words, x_scales, w1, w2, unit, w3, of
         ask2_sb = keep.tile([P, U // LIST_ROWS], U16)
         xw = keep.tile([P, T], I32, align_bytes=64)
         xs = keep.tile([P, T], U8, align_bytes=64)
-        w2_raw = keep.tile([P, PACK, H], F32, name="shared_raw")
+        w2_raw = keep.tile([P, PACK, H], F32)
+        w3_raw = keep.tile([P, PACK, N], F32)
         w1_raw = keep.tile([P, PACK, H], F32)
         unit_sb = keep.tile([P, PACK], F32)
 
@@ -51,6 +52,7 @@ def tile_picked_ypeerlo_spr_p_kernel(tc, x_words, x_scales, w1, w2, unit, w3, of
         nc.sync.dma_start(xw[:], x_words[0].rearrange("p n t -> p (n t)").bitcast(I32))
         nc.sync.dma_start(ask1_sb[:], ask1)
         nc.sync.dma_start(ask2_sb[:], ask2)
+        nc.sync.dma_start(w3_raw[:], w3.rearrange("(p t) n -> p t n", t=PACK))
         nc.sync.dma_start(w1_raw[:], w1.rearrange("(p j) c -> p j c", j=PACK))
 
         z_win = [keep.tile([P, WINDOW], F32, name="z" + str(t)) for t in range(PACK)]
@@ -71,23 +73,17 @@ def tile_picked_ypeerlo_spr_p_kernel(tc, x_words, x_scales, w1, w2, unit, w3, of
         xg_scales = keep.tile([P, S], U8, align_bytes=64)
         xg_words = keep.tile([P, S], U32, align_bytes=64)
 
-        def weight_tiles(name):
-            grouped = keep.tile([P, PACK, P, PACK], BF16, align_bytes=64, name=name + "_bf")
-            codes = keep.tile([P, H], U32, align_bytes=64, name=name + "_codes")
-            scales = keep.tile([P, H], U8, align_bytes=64, name=name + "_scales")
-            return grouped, codes, scales
-
-        def cast_weight(copy, raw, grouped, t0, t1):
+        def cast_weight(copy, raw, grouped, t0):
             copy(
-                grouped[:, t0:t1].rearrange("p t m j -> p m j t"),
-                raw[:].rearrange("p j (m t) -> p m j t", t=PACK)[:, :, :, t0:t1],
+                grouped[:].rearrange("p t m j -> p m j t"),
+                raw[:].rearrange("p j (m t) -> p m j t", t=PACK)[:, :, :, t0 : t0 + 2],
             )
 
-        def quantise_weight(grouped, codes, scales, t0, t1):
+        def quantise_weight(grouped, codes, scales, t0):
             nc.vector.quantize_mx(
-                out=codes[:, t0 * P : t1 * P].bitcast(FP8X4),
-                scales=scales[:, t0 * P : t1 * P],
-                in_=grouped[:, t0:t1].rearrange("p t m j -> p (t m j)"),
+                out=codes[:, t0 * P : (t0 + 2) * P].bitcast(FP8X4),
+                scales=scales[:, t0 * P : (t0 + 2) * P],
+                in_=grouped[:].rearrange("p t m j -> p (t m j)"),
             )
 
         def product(codes, scales, t, cols):
@@ -109,12 +105,20 @@ def tile_picked_ypeerlo_spr_p_kernel(tc, x_words, x_scales, w1, w2, unit, w3, of
         def entries(lst, r0, n):
             return lst[:, r0 // LIST_ROWS : (r0 + n) // LIST_ROWS]
 
-        w2_bf, w2_codes, w2_scales = weight_tiles("w2")
-        w1_bf, w1_codes, w1_scales = weight_tiles("w1")
-        cast_weight(nc.vector.tensor_copy, w2_raw, w2_bf, 0, 2)
-        cast_weight(nc.scalar.copy, w2_raw, w2_bf, 2, PACK)
+        w2_codes = keep.tile([P, H], U32, align_bytes=64)
+        w2_scales = keep.tile([P, H], U8, align_bytes=64)
+        w1_codes = keep.tile([P, H], U32, align_bytes=64)
+        w1_scales = keep.tile([P, H], U8, align_bytes=64)
+        w2_bf = keep.tile([P, PACK, P, PACK], BF16, align_bytes=64)
+        w1_bf = [pair.tile([P, 2, P, PACK], BF16, align_bytes=64, name="low") for h in range(2)]
+        w2_from = w2_raw[:].rearrange("p j (m t) -> p m j t", t=PACK)
+        w2_to = w2_bf[:].rearrange("p t m j -> p m j t")
+        nc.vector.tensor_copy(w2_to[:, :48], w2_from[:, :48])
+        nc.scalar.copy(w2_to[:, 48:], w2_from[:, 48:])
         nc.vector.tensor_copy(xg_scales[:], xs[:].indirect(offs_sb[:]))
-        quantise_weight(w2_bf, w2_codes, w2_scales, 0, PACK)
+        nc.vector.quantize_mx(
+            out=w2_codes[:].bitcast(FP8X4), scales=w2_scales[:], in_=w2_bf[:].rearrange("p t m j -> p (t m j)")
+        )
         for half in range(2):
             cols = slice(half * S // 2, (half + 1) * S // 2)
             picks = entries(offs_sb, half * S // 2, S // 2)
@@ -123,32 +127,24 @@ def tile_picked_ypeerlo_spr_p_kernel(tc, x_words, x_scales, w1, w2, unit, w3, of
             nc.scalar.activation(z_win[0][:, cols], acc[:, cols], COPY, scale=neg_size[:, 0:1])
         every = slice(0, S)
         z_acc = {t: product(w2_codes, w2_scales, t, every) for t in range(1, PACK)}
-        nc.vector.tensor_scalar(z_win[1][:, :S], z_acc[1][:], neg_size[:, 1:2], None, ALU.mult)
-        cast_weight(nc.vector.tensor_copy, w1_raw, w1_bf, 0, 1)
-        quantise_weight(w1_bf, w1_codes, w1_scales, 0, 1)
-        y_acc = {0: product(w1_codes, w1_scales, 0, every)}
-        cast_weight(nc.vector.tensor_copy, w1_raw, w1_bf, 1, PACK)
-        nc.vector.tensor_scalar(y_win[0][:, :S], y_acc[0][:], size[:, 0:1], None, ALU.mult)
-        quantise_weight(w1_bf, w1_codes, w1_scales, 1, PACK)
-        for t in range(1, PACK):
-            y_acc[t] = product(w1_codes, w1_scales, t, every)
-
-        w3_raw = keep.tile([P, PACK, N], F32, name="shared_raw")
-        nc.sync.dma_start(w3_raw[:], w3.rearrange("(p t) n -> p t n", t=PACK))
         w3_bf = keep.tile([P, N, PACK], BF16, align_bytes=64)
         w3_codes = keep.tile([P, N], U32, align_bytes=64)
         w3_scales = keep.tile([P, N], U8, align_bytes=64)
-
-        def prepare_w3():
-            nc.vector.tensor_tensor(
-                w3_bf[:].rearrange("p (c e) t -> p c t e", e=2),
-                w3_raw[:].rearrange("p t (c e) -> p c t e", e=2),
-                sgn[:].unsqueeze(1).unsqueeze(3).to_broadcast([P, N // 2, PACK, 2]),
-                ALU.mult,
-            )
-            nc.vector.quantize_mx(
-                out=w3_codes[:].bitcast(FP8X4), scales=w3_scales[:], in_=w3_bf[:].rearrange("p n t -> p (n t)")
-            )
+        nc.vector.tensor_tensor(
+            w3_bf[:].rearrange("p (c e) t -> p c t e", e=2),
+            w3_raw[:].rearrange("p t (c e) -> p c t e", e=2),
+            sgn[:].unsqueeze(1).unsqueeze(3).to_broadcast([P, N // 2, PACK, 2]),
+            ALU.mult,
+        )
+        nc.vector.quantize_mx(
+            out=w3_codes[:].bitcast(FP8X4), scales=w3_scales[:], in_=w3_bf[:].rearrange("p n t -> p (n t)")
+        )
+        nc.vector.tensor_scalar(z_win[1][:, :S], z_acc[1][:], neg_size[:, 1:2], None, ALU.mult)
+        cast_weight(nc.vector.tensor_copy, w1_raw, w1_bf[0], 0)
+        cast_weight(nc.vector.tensor_copy, w1_raw, w1_bf[1], 2)
+        quantise_weight(w1_bf[0], w1_codes, w1_scales, 0)
+        quantise_weight(w1_bf[1], w1_codes, w1_scales, 2)
+        y_acc = [product(w1_codes, w1_scales, t, every) for t in range(PACK)]
 
         hid_bf = keep.tile([P, U, PACK], BF16, align_bytes=64)
         hid_codes = keep.tile([P, U], U32, align_bytes=64)
@@ -169,7 +165,7 @@ def tile_picked_ypeerlo_spr_p_kernel(tc, x_words, x_scales, w1, w2, unit, w3, of
                 in_=hid_bf[:, r0 : r0 + n, :].rearrange("p n t -> p (n t)"),
             )
 
-        def finish(r0, n):
+        def finish(r0, n, copy, queue):
             acc = psum.tile([P, S], F32, name="acc")
             cols = slice(r0, r0 + n)
             nc.tensor.matmul_mx(
@@ -182,56 +178,63 @@ def tile_picked_ypeerlo_spr_p_kernel(tc, x_words, x_scales, w1, w2, unit, w3, of
                 stop=True,
             )
             staged = keep.tile([P, n], F32, name="staged" + str(r0))
-            nc.scalar.copy(staged[:], acc[:, :n])
-            nc.sync.dma_start(out[:, cols], staged[:])
+            copy(staged[:], acc[:, :n])
+            queue.dma_start(out[:, cols], staged[:])
 
         first = keep.tile([P, PACK, FUSED], F32)
         second = keep.tile([P, PACK, FUSED], F32)
 
-        def fused_piece(t, r0, n):
+        def lowest_bid(t, r0, n):
+            if t == 3:
+                evict(z_win, z_acc, neg_size, t)
             bids = ring.tile([P, 2, n], F32, name="fetched")
             nc.scalar.activation(bids[:, 0, :], z_win[t][:].indirect(entries(ask1_sb, r0, n)), COPY)
+            if t == 1:
+                evict(z_win, z_acc, neg_size, 2)
             nc.scalar.activation(bids[:, 1, :], z_win[t][:].indirect(entries(ask2_sb, r0, n)), COPY)
-            if r0 == 0 and t > 0:
+            if t > 2:
                 evict(y_win, y_acc, size, t)
-            low = pair.tile([P, n], F32, name="low")
+            low = pair.tile([P, n], F32, align_bytes=64, name="low")
             nc.vector.tensor_tensor(low[:], bids[:, 0, :], bids[:, 1, :], ALU.min)
-            cols = slice(r0, r0 + n)
-            nc.vector.tensor_tensor(first[:, t, cols], y_win[t][:].indirect(entries(ask1_sb, r0, n)), low[:], ALU.add)
-            nc.vector.tensor_tensor(second[:, t, cols], y_win[t][:].indirect(entries(ask2_sb, r0, n)), low[:], ALU.add)
+            return low
 
-        for t in range(PACK):
-            if t > 1:
-                evict(z_win, z_acc, neg_size, t)
-            if t == 0:
-                fused_piece(t, 0, FIRST_PIECE)
-                fused_piece(t, FIRST_PIECE, FUSED - FIRST_PIECE)
-                prepare_w3()
-            else:
-                fused_piece(t, 0, FUSED)
+        def fetch_and_add(target, lst, t, r0, n, low):
+            window = y_win[t][:].indirect(entries(lst, r0, n))
+            nc.vector.tensor_tensor(target[:, t, r0 : r0 + n], window, low[:], ALU.add)
 
-        lows = keep.tile([P, PACK, 2, COPIED], F32)
-
-        def copied_piece(t):
+        def copied_piece(lows, t):
             both = ring.tile([P, 2, 2, COPIED], F32, name="fetched")
             for which, win in enumerate((z_win, y_win)):
                 for side, lst in enumerate((ask1_sb, ask2_sb)):
                     nc.scalar.activation(both[:, side, which, :], win[t][:].indirect(entries(lst, FUSED, COPIED)), COPY)
             nc.vector.tensor_tensor(lows[:, t], both[:, 0], both[:, 1], ALU.min)
 
-        combine(first[:, :, :512], second[:, :, :512], ALU.min, 0, 512)
-        copied_piece(0)
-        copied_piece(1)
+        steps = [(0, 0, FIRST_PIECE), (0, FIRST_PIECE, FUSED - FIRST_PIECE)] + [(t, 0, FUSED) for t in range(1, PACK)]
+        low = lowest_bid(*steps[0])
+        for t in range(3):
+            nc.vector.tensor_scalar(y_win[t][:, :S], y_acc[t][:], size[:, t : t + 1], None, ALU.mult)
+        for i, step in enumerate(steps):
+            fetch_and_add(first, ask1_sb, *step, low)
+            if i + 1 < len(steps):
+                next_low = lowest_bid(*steps[i + 1])
+            else:
+                lows = pair.tile([P, PACK, 2, COPIED], F32, align_bytes=64, name="low")
+                copied_piece(lows, 0)
+            fetch_and_add(second, ask2_sb, *step, low)
+            low = next_low
+
+        copied_piece(lows, 1)
+        combine(first[:], second[:], ALU.min, 0, FUSED)
+        copied_piece(lows, 2)
         quantise_hid(0, 512)
-        combine(first[:, :, 512:], second[:, :, 512:], ALU.min, 512, 256)
-        copied_piece(2)
-        quantise_hid(512, 256)
-        copied_piece(3)
-        finish(0, 512)
-        finish(512, 256)
-        combine(lows[:, :, 0, :128], lows[:, :, 1, :128], ALU.add, 768, 128)
-        combine(lows[:, :, 0, 128:], lows[:, :, 1, 128:], ALU.add, 896, 128)
-        quantise_hid(768, 128)
+        quantise_hid(512, 128)
+        copied_piece(lows, 3)
+        finish(0, 512, nc.scalar.copy, nc.sync)
+        finish(512, 128, nc.scalar.copy, nc.sync)
+        cut = 896 - FUSED
+        combine(lows[:, :, 0, :cut], lows[:, :, 1, :cut], ALU.add, FUSED, cut)
+        combine(lows[:, :, 0, cut:], lows[:, :, 1, cut:], ALU.add, 896, 128)
+        quantise_hid(640, 256)
         quantise_hid(896, 128)
-        finish(768, 128)
-        finish(896, 128)
+        finish(640, 256, nc.scalar.copy, nc.scalar)
+        finish(896, 128, nc.vector.tensor_copy, nc.sync)

from contextlib import ExitStack

import concourse.mybir as mybir

F32 = mybir.dt.float32
BF16 = mybir.dt.bfloat16
I32 = mybir.dt.int32
U32 = mybir.dt.uint32
U16 = mybir.dt.uint16
U8 = mybir.dt.uint8
FP8X4 = mybir.dt.float8_e4m3fn_x4
ALU = mybir.AluOpType
COPY = mybir.ActivationFunctionType.Copy

K, T, S, N, H, U = 512, 2048, 512, 128, 512, 1024
FLOPS = 2 * (2 * K * H * S + H * N * U)

P = 128
PACK = 4
LIST_ROWS = 16

FUSED = 736
COPIED = U - FUSED
WINDOW = FUSED + LIST_ROWS
FIRST_PIECE = 384


def tile_picked_ypeerlo_spr_p_kernel(tc, x_words, x_scales, w1, w2, unit, w3, offs, ask1, ask2, out):
    nc = tc.nc
    with ExitStack() as ctx:
        keep = ctx.enter_context(tc.tile_pool(name="keep", bufs=1))
        ring = ctx.enter_context(tc.tile_pool(name="ring", bufs=3))
        pair = ctx.enter_context(tc.tile_pool(name="pair", bufs=2))
        psum = ctx.enter_context(tc.psum_pool(name="psum", bufs=8))

        offs_sb = keep.tile([P, S // LIST_ROWS], U16)
        ask1_sb = keep.tile([P, U // LIST_ROWS], U16)
        ask2_sb = keep.tile([P, U // LIST_ROWS], U16)
        xw = keep.tile([P, T], I32, align_bytes=64)
        xs = keep.tile([P, T], U8, align_bytes=64)
        w2_raw = keep.tile([P, PACK, H], F32)
        w3_raw = keep.tile([P, PACK, N], F32)
        w1_raw = keep.tile([P, PACK, H], F32)
        unit_sb = keep.tile([P, PACK], F32)

        nc.gpsimd.memset(xs[:].bitcast(I32), 0)
        nc.sync.dma_start(offs_sb[:], offs)
        nc.scalar.dma_start(unit_sb[:], unit.rearrange("(p t) o -> p (t o)", t=PACK))
        nc.sync.dma_start(w2_raw[:], w2.rearrange("(p j) c -> p j c", j=PACK))
        for q in range(4):
            nc.sync.dma_start(xs[32 * q : 32 * q + 4, :].bitcast(I32), x_scales[0, 4 * q : 4 * q + 4, :].bitcast(I32))
        nc.sync.dma_start(xw[:], x_words[0].rearrange("p n t -> p (n t)").bitcast(I32))
        nc.sync.dma_start(ask1_sb[:], ask1)
        nc.sync.dma_start(ask2_sb[:], ask2)
        nc.sync.dma_start(w3_raw[:], w3.rearrange("(p t) n -> p t n", t=PACK))
        nc.sync.dma_start(w1_raw[:], w1.rearrange("(p j) c -> p j c", j=PACK))

        z_win = [keep.tile([P, WINDOW], F32, name="z" + str(t)) for t in range(PACK)]
        y_win = [keep.tile([P, WINDOW], F32, name="y" + str(t)) for t in range(PACK)]
        for t in range(PACK):
            nc.gpsimd.memset(z_win[t][:, S:], 0.0)
            nc.gpsimd.memset(y_win[t][:, S:], 0.0)

        size = keep.tile([P, PACK], F32)
        neg_size = keep.tile([P, PACK], F32)
        twice = keep.tile([P, PACK], F32)
        sgn = keep.tile([P, PACK], F32)
        nc.vector.scalar_tensor_tensor(neg_size[:], unit_sb[:], -1.0, unit_sb[:], ALU.mult, ALU.min)
        nc.vector.scalar_tensor_tensor(size[:], unit_sb[:], -1.0, unit_sb[:], ALU.mult, ALU.max)
        nc.vector.tensor_scalar(twice[:], unit_sb[:], 0.0, 2.0, ALU.is_ge, ALU.mult)
        nc.vector.tensor_scalar(sgn[:], twice[:], 1.0, -1.0, ALU.mult, ALU.add)

        xg_scales = keep.tile([P, S], U8, align_bytes=64)
        xg_words = keep.tile([P, S], U32, align_bytes=64)

        def cast_weight(copy, raw, grouped, t0):
            copy(
                grouped[:].rearrange("p t m j -> p m j t"),
                raw[:].rearrange("p j (m t) -> p m j t", t=PACK)[:, :, :, t0 : t0 + 2],
            )

        def quantise_weight(grouped, codes, scales, t0):
            nc.vector.quantize_mx(
                out=codes[:, t0 * P : (t0 + 2) * P].bitcast(FP8X4),
                scales=scales[:, t0 * P : (t0 + 2) * P],
                in_=grouped[:].rearrange("p t m j -> p (t m j)"),
            )

        def product(codes, scales, t, cols):
            acc = psum.tile([P, S], F32, name="acc")
            nc.tensor.matmul_mx(
                out=acc[:, cols],
                lhsT=codes[:, t * P : (t + 1) * P].bitcast(FP8X4),
                lhsT_scale=scales[:, t * P : (t + 1) * P],
                rhs=xg_words[:, cols].bitcast(FP8X4),
                rhs_scale=xg_scales[:, cols],
                start=True,
                stop=True,
            )
            return acc

        def evict(window, acc, factor, t):
            nc.scalar.activation(window[t][:, :S], acc[t][:], COPY, scale=factor[:, t : t + 1])

        def entries(lst, r0, n):
            return lst[:, r0 // LIST_ROWS : (r0 + n) // LIST_ROWS]

        w2_codes = keep.tile([P, H], U32, align_bytes=64)
        w2_scales = keep.tile([P, H], U8, align_bytes=64)
        w1_codes = keep.tile([P, H], U32, align_bytes=64)
        w1_scales = keep.tile([P, H], U8, align_bytes=64)
        w2_bf = keep.tile([P, PACK, P, PACK], BF16, align_bytes=64)
        w1_bf = [pair.tile([P, 2, P, PACK], BF16, align_bytes=64, name="low") for h in range(2)]
        w2_from = w2_raw[:].rearrange("p j (m t) -> p m j t", t=PACK)
        w2_to = w2_bf[:].rearrange("p t m j -> p m j t")
        nc.vector.tensor_copy(w2_to[:, :48], w2_from[:, :48])
        nc.scalar.copy(w2_to[:, 48:], w2_from[:, 48:])
        nc.vector.tensor_copy(xg_scales[:], xs[:].indirect(offs_sb[:]))
        nc.vector.quantize_mx(
            out=w2_codes[:].bitcast(FP8X4), scales=w2_scales[:], in_=w2_bf[:].rearrange("p t m j -> p (t m j)")
        )
        for half in range(2):
            cols = slice(half * S // 2, (half + 1) * S // 2)
            picks = entries(offs_sb, half * S // 2, S // 2)
            nc.vector.tensor_copy(xg_words[:, cols], xw[:].bitcast(U32).indirect(picks))
            acc = product(w2_codes, w2_scales, 0, cols)
            nc.scalar.activation(z_win[0][:, cols], acc[:, cols], COPY, scale=neg_size[:, 0:1])
        every = slice(0, S)
        z_acc = {t: product(w2_codes, w2_scales, t, every) for t in range(1, PACK)}
        w3_bf = keep.tile([P, N, PACK], BF16, align_bytes=64)
        w3_codes = keep.tile([P, N], U32, align_bytes=64)
        w3_scales = keep.tile([P, N], U8, align_bytes=64)
        nc.vector.tensor_tensor(
            w3_bf[:].rearrange("p (c e) t -> p c t e", e=2),
            w3_raw[:].rearrange("p t (c e) -> p c t e", e=2),
            sgn[:].unsqueeze(1).unsqueeze(3).to_broadcast([P, N // 2, PACK, 2]),
            ALU.mult,
        )
        nc.vector.quantize_mx(
            out=w3_codes[:].bitcast(FP8X4), scales=w3_scales[:], in_=w3_bf[:].rearrange("p n t -> p (n t)")
        )
        nc.vector.tensor_scalar(z_win[1][:, :S], z_acc[1][:], neg_size[:, 1:2], None, ALU.mult)
        cast_weight(nc.vector.tensor_copy, w1_raw, w1_bf[0], 0)
        cast_weight(nc.vector.tensor_copy, w1_raw, w1_bf[1], 2)
        quantise_weight(w1_bf[0], w1_codes, w1_scales, 0)
        quantise_weight(w1_bf[1], w1_codes, w1_scales, 2)
        y_acc = [product(w1_codes, w1_scales, t, every) for t in range(PACK)]

        hid_bf = keep.tile([P, U, PACK], BF16, align_bytes=64)
        hid_codes = keep.tile([P, U], U32, align_bytes=64)
        hid_scales = keep.tile([P, U], U8, align_bytes=64)

        def combine(left, right, op, r0, n):
            nc.vector.tensor_tensor(
                hid_bf[:, r0 : r0 + n, :].rearrange("p (c e) t -> p c t e", e=2),
                left.rearrange("p t (c e) -> p c t e", e=2),
                right.rearrange("p t (c e) -> p c t e", e=2),
                op,
            )

        def quantise_hid(r0, n):
            nc.vector.quantize_mx(
                out=hid_codes[:, r0 : r0 + n].bitcast(FP8X4),
                scales=hid_scales[:, r0 : r0 + n],
                in_=hid_bf[:, r0 : r0 + n, :].rearrange("p n t -> p (n t)"),
            )

        def finish(r0, n, copy, queue):
            acc = psum.tile([P, S], F32, name="acc")
            cols = slice(r0, r0 + n)
            nc.tensor.matmul_mx(
                out=acc[:, :n],
                lhsT=w3_codes[:].bitcast(FP8X4),
                lhsT_scale=w3_scales[:],
                rhs=hid_codes[:, cols].bitcast(FP8X4),
                rhs_scale=hid_scales[:, cols],
                start=True,
                stop=True,
            )
            staged = keep.tile([P, n], F32, name="staged" + str(r0))
            copy(staged[:], acc[:, :n])
            queue.dma_start(out[:, cols], staged[:])

        first = keep.tile([P, PACK, FUSED], F32)
        second = keep.tile([P, PACK, FUSED], F32)

        def lowest_bid(t, r0, n):
            if t == 3:
                evict(z_win, z_acc, neg_size, t)
            bids = ring.tile([P, 2, n], F32, name="fetched")
            nc.scalar.activation(bids[:, 0, :], z_win[t][:].indirect(entries(ask1_sb, r0, n)), COPY)
            if t == 1:
                evict(z_win, z_acc, neg_size, 2)
            nc.scalar.activation(bids[:, 1, :], z_win[t][:].indirect(entries(ask2_sb, r0, n)), COPY)
            if t > 2:
                evict(y_win, y_acc, size, t)
            low = pair.tile([P, n], F32, align_bytes=64, name="low")
            nc.vector.tensor_tensor(low[:], bids[:, 0, :], bids[:, 1, :], ALU.min)
            return low

        def fetch_and_add(target, lst, t, r0, n, low):
            window = y_win[t][:].indirect(entries(lst, r0, n))
            nc.vector.tensor_tensor(target[:, t, r0 : r0 + n], window, low[:], ALU.add)

        def copied_piece(lows, t):
            both = ring.tile([P, 2, 2, COPIED], F32, name="fetched")
            for which, win in enumerate((z_win, y_win)):
                for side, lst in enumerate((ask1_sb, ask2_sb)):
                    nc.scalar.activation(both[:, side, which, :], win[t][:].indirect(entries(lst, FUSED, COPIED)), COPY)
            nc.vector.tensor_tensor(lows[:, t], both[:, 0], both[:, 1], ALU.min)

        steps = [(0, 0, FIRST_PIECE), (0, FIRST_PIECE, FUSED - FIRST_PIECE)] + [(t, 0, FUSED) for t in range(1, PACK)]
        low = lowest_bid(*steps[0])
        for t in range(3):
            nc.vector.tensor_scalar(y_win[t][:, :S], y_acc[t][:], size[:, t : t + 1], None, ALU.mult)
        for i, step in enumerate(steps):
            fetch_and_add(first, ask1_sb, *step, low)
            if i + 1 < len(steps):
                next_low = lowest_bid(*steps[i + 1])
            else:
                lows = pair.tile([P, PACK, 2, COPIED], F32, align_bytes=64, name="low")
                copied_piece(lows, 0)
            fetch_and_add(second, ask2_sb, *step, low)
            low = next_low

        copied_piece(lows, 1)
        combine(first[:], second[:], ALU.min, 0, FUSED)
        copied_piece(lows, 2)
        quantise_hid(0, 512)
        quantise_hid(512, 128)
        copied_piece(lows, 3)
        finish(0, 512, nc.scalar.copy, nc.sync)
        finish(512, 128, nc.scalar.copy, nc.sync)
        cut = 896 - FUSED
        combine(lows[:, :, 0, :cut], lows[:, :, 1, :cut], ALU.add, FUSED, cut)
        combine(lows[:, :, 0, cut:], lows[:, :, 1, cut:], ALU.add, 896, 128)
        quantise_hid(640, 256)
        quantise_hid(896, 128)
        finish(640, 256, nc.scalar.copy, nc.scalar)
        finish(896, 128, nc.vector.tensor_copy, nc.sync)
